import numpy as np, ml_dtypes
CORES = [33,34,161,162,289,290,417,418]
N = 8
import mx_ref
KT = 1
BF = ml_dtypes.bfloat16
def setup_inputs(rng):
    def f(*shape):
        return mx_ref.flush((rng.standard_normal(shape, dtype=np.float32) * np.exp2(rng.integers(-2, 3, shape[:-1] + (1,)))).astype(BF))
    return {"x": f(N, 128, KT * 512)}
def setup_inputs_blocks(rng):
    d = setup_inputs(rng)
    for k in ("x",): d[k] = mx_ref.spread(d[k], rng, 4)
    return d
def setup_inputs_wide(rng):
    d = setup_inputs(rng)
    for k in ("x",): d[k] = mx_ref.flush((d[k].astype(np.float32) * np.exp2(rng.integers(-8, 9, (N, 1, 1))).astype(np.float32)).astype(BF))
    return d
def setup_inputs_zeros(rng):
    d = setup_inputs(rng); v = d["x"].reshape(N, 128, -1, 4).copy()
    v[np.broadcast_to((rng.random((N, 1, v.shape[2], 1)) < 0.33), v.shape)] = 0
    d["x"] = v.reshape(d["x"].shape)
    return d
def reference(x):
    Q = [[mx_ref.quantize(x[j][:, 512 * t:512 * t + 512]) for t in range(KT)] for j in range(N)]
    y = np.zeros((N, 128, N * 128), np.float32)
    for r in range(N):
        for j in range(N):
            for t in range(KT):
                p = mx_ref.matmul(Q[r][t], Q[j][t])
                y[r][:, 128 * j:128 * j + 128] = p if t == 0 else y[r][:, 128 * j:128 * j + 128] + p
    return {"y": y}

@@ -1,0 +1,129 @@
+from concourse.bass import DstId, RemoteDMATransfer
+from concourse.mybir import dt
+
+N = 8
+W = 128
+NG = 6
+
+SCRATCH = {
+    "xb": ("sbuf", [128, 4 * W], "bfloat16"),
+    "q": ("sbuf", [128, N * W], "float8_e4m3fn_x4"),
+    "s": ("sbuf", [128, N * W], "uint8"),
+    "ps": ("psum", [128, 512 * NG], "float32"),
+    "yb": ("sbuf", [128, N * W], "float32"),
+}
+SEMAPHORES = (["ld", "qd", "sent", "st_a", "st_b"]
+              + ["c%d" % j for j in range(N)] + ["p%d" % j for j in range(N)]
+              + ["mm%d" % k for k in range(NG)] + ["cp%d" % k for k in range(NG)])
+
+
+def _bits(m):
+    return [e for e in range(m.bit_length()) if (m >> e) & 1]
+
+
+def _mask(engines):
+    m = 0
+    for e in engines:
+        m |= 1 << e
+    return m
+
+
+def _plan(cores, topo):
+    by_host = {}
+    for r, c in enumerate(cores):
+        by_host.setdefault(topo.host(c), []).append(r)
+    steps = ({r: [] for r in range(len(cores))}, {r: [] for r in range(len(cores))})
+    info = {}
+    for r, c in enumerate(cores):
+        h = topo.host(c)
+        slot = by_host[h].index(r)
+        peer = by_host[h][1 - slot]
+        near = [k for k in by_host if k != h and topo.may_write(c, cores[by_host[k][slot]])
+                and topo.rack(k) == topo.rack(h)][0]
+        far = [k for k in by_host if k != h and topo.may_write(c, cores[by_host[k][slot]])
+               and topo.rack(k) != topo.rack(h)][0]
+        leave = _bits(topo.mask(c, cores[by_host[near][slot]]) & topo.mask(c, cores[by_host[far][slot]]))
+        stay = [e for e in _bits(topo.mask(c, cores[peer])) if e not in leave]
+        m_near, m_far = _mask(leave[0::2]), _mask(leave[1::2])
+        half = len(stay) // 2
+        steps[0][r] += [(r, by_host[near][slot], m_near), (r, by_host[far][slot], m_far), (r, peer, _mask(stay))]
+        t_near, t_far = by_host[near][slot], by_host[far][slot]
+        steps[1][r] += [(t_near, by_host[far][slot], m_far), (t_far, by_host[near][1 - slot], m_near),
+                        (t_near, peer, _mask(stay[:half])), (t_far, peer, _mask(stay[half:]))]
+        diag = [k for k in by_host if k not in (h, near, far)][0]
+        info[r] = (sorted(by_host[h]), t_near, t_far, by_host[near][1 - slot], by_host[far][1 - slot],
+                   sorted(by_host[diag]))
+    return steps, info
+
+
+def rank_program(g, core, T, topo):
+    r = T.rank_of(core)
+    if r is None:
+        return
+    cores = list(T.cores)
+    steps, info = _plan(cores, topo)
+    home, t_near, t_far, u_near, u_far, diag = info[r]
+
+    lands = {}
+    for step in steps:
+        for sender in step:
+            for tile, dst, m in step[sender]:
+                if dst == r:
+                    lands[tile] = len(_bits(m))
+
+    def codes(j, n=1):
+        return T.q[:, j * W:(j + n) * W]
+
+    def plane(j, n=1):
+        return T.s[:, j * W:(j + n) * W]
+
+    g.sync.dma_start(T.xb[:], T.x[:]).then_inc(T.sem.ld, 16)
+    g.vector.wait_ge(T.sem.ld, 16)
+    g.vector.quantize_mx(codes(r), plane(r), T.xb[:]).then_inc(T.sem.qd, 1)
+
+    left = [0]
+
+    def send(step, what):
+        trs = []
+        for tile, dst, m in steps[step][r]:
+            rid, pid = topo.addr(cores[dst], core)
+            if what == "c":
+                ap = codes(tile).bitcast(dt.uint8)
+            else:
+                ap = plane(tile)
+            trs.append(RemoteDMATransfer(dst_ids=[DstId(rid=rid, pnc=pid)], dma_engine_mask=m,
+                                         remote_sem=T.sem["%s%d" % (what, tile)], src=ap, dst=ap))
+            left[0] += len(_bits(m))
+        g.remote_dma_fused(trs, local_sem=T.sem.sent)
+
+    g.wait_ge(T.sem.qd, 1)
+    send(0, "c")
+    send(0, "p")
+    for what in ("c", "p"):
+        for t in (t_near, t_far):
+            g.wait_ge(T.sem["%s%d" % (what, t)], lands[t])
+        send(1, what)
+    g.wait_ge(T.sem.sent, left[0])
+
+    def merged(pair):
+        return [pair] if pair[1] == pair[0] + 1 else [[pair[0]], [pair[1]]]
+
+    groups = merged(home) + [[t_near], [t_far], [u_near], [u_far]] + merged(diag)
+    stores = {"st_a": 0, "st_b": 0}
+    g.tensor.wait_ge(T.sem.qd, 1)
+    for k, tiles in enumerate(groups):
+        a, n = tiles[0], len(tiles)
+        for j in tiles:
+            if j != r:
+                g.tensor.wait_ge(T.sem["c%d" % j], lands[j])
+                g.tensor.wait_ge(T.sem["p%d" % j], lands[j])
+        bank = T.ps[:, 512 * k:512 * k + n * W]
+        g.tensor.matmul_mx(bank, codes(r), plane(r), codes(a, n), plane(a, n), True, True).then_inc(T.sem["mm%d" % k], 1)
+        g.vector.wait_ge(T.sem["mm%d" % k], 1)
+        g.vector.tensor_copy(T.yb[:, a * W:(a + n) * W], bank).then_inc(T.sem["cp%d" % k], 1)
+        queue, name = ((g.sync, "st_a"), (g.scalar, "st_b"))[k % 2]
+        queue.wait_ge(T.sem["cp%d" % k], 1)
+        queue.dma_start(T.y[:, a * W:(a + n) * W], T.yb[:, a * W:(a + n) * W]).then_inc(T.sem[name], 16)
+        stores[name] += 16
+    g.sync.wait_ge(T.sem.st_a, stores["st_a"])
+    g.scalar.wait_ge(T.sem.st_b, stores["st_b"])

@@ -1,9 +1,9 @@
 from concourse.bass import DstId, RemoteDMATransfer
-from concourse.mybir import dt
+from concourse.mybir import dt, ActivationFunctionType
 
 N = 8
 W = 128
-NG = 6
+NG = 5
 
 SCRATCH = {
     "xb": ("sbuf", [128, 4 * W], "bfloat16"),
@@ -12,7 +12,7 @@ SCRATCH = {
     "ps": ("psum", [128, 512 * NG], "float32"),
     "yb": ("sbuf", [128, N * W], "float32"),
 }
-SEMAPHORES = (["ld", "qd", "sent", "st_a", "st_b"]
+SEMAPHORES = (["ld", "qd", "sent", "gone", "st_a", "st_b"]
               + ["c%d" % j for j in range(N)] + ["p%d" % j for j in range(N)]
               + ["mm%d" % k for k in range(NG)] + ["cp%d" % k for k in range(NG)])
 
@@ -32,28 +32,29 @@ def _plan(cores, topo):
     by_host = {}
     for r, c in enumerate(cores):
         by_host.setdefault(topo.host(c), []).append(r)
-    steps = ({r: [] for r in range(len(cores))}, {r: [] for r in range(len(cores))})
-    info = {}
+    calls, place = {}, {}
     for r, c in enumerate(cores):
         h = topo.host(c)
         slot = by_host[h].index(r)
         peer = by_host[h][1 - slot]
-        near = [k for k in by_host if k != h and topo.may_write(c, cores[by_host[k][slot]])
-                and topo.rack(k) == topo.rack(h)][0]
-        far = [k for k in by_host if k != h and topo.may_write(c, cores[by_host[k][slot]])
-               and topo.rack(k) != topo.rack(h)][0]
+        open_to = [k for k in by_host if k != h and topo.may_write(c, cores[by_host[k][slot]])]
+        near = [k for k in open_to if topo.rack(k) == topo.rack(h)][0]
+        far = [k for k in open_to if topo.rack(k) != topo.rack(h)][0]
+        diag = [k for k in by_host if k not in (h, near, far)][0]
         leave = _bits(topo.mask(c, cores[by_host[near][slot]]) & topo.mask(c, cores[by_host[far][slot]]))
         stay = [e for e in _bits(topo.mask(c, cores[peer])) if e not in leave]
-        m_near, m_far = _mask(leave[0::2]), _mask(leave[1::2])
-        half = len(stay) // 2
-        steps[0][r] += [(r, by_host[near][slot], m_near), (r, by_host[far][slot], m_far), (r, peer, _mask(stay))]
+        m_near, m_far, m_stay = _mask(leave[0::2]), _mask(leave[1::2]), _mask(stay)
         t_near, t_far = by_host[near][slot], by_host[far][slot]
-        steps[1][r] += [(t_near, by_host[far][slot], m_far), (t_far, by_host[near][1 - slot], m_near),
-                        (t_near, peer, _mask(stay[:half])), (t_far, peer, _mask(stay[half:]))]
-        diag = [k for k in by_host if k not in (h, near, far)][0]
-        info[r] = (sorted(by_host[h]), t_near, t_far, by_host[near][1 - slot], by_host[far][1 - slot],
-                   sorted(by_host[diag]))
-    return steps, info
+        calls[r] = {
+            "own_out": [(r, 1, t_near, m_near), (r, 1, t_far, m_far)],
+            "own_chip": [(r, 1, peer, m_stay)],
+            "relay_cable": [(t_near, 1, t_far, m_far)],
+            "relay_switch": [(t_far, 1, by_host[near][1 - slot], m_near)],
+            "pair_chip": [(t_near, 2, peer, m_stay)],
+        }
+        place[r] = (sorted(by_host[h]) + [t_near, t_far, by_host[near][1 - slot], by_host[far][1 - slot]]
+                    + sorted(by_host[diag]))
+    return calls, place
 
 
 def rank_program(g, core, T, topo):
@@ -61,69 +62,88 @@ def rank_program(g, core, T, topo):
     if r is None:
         return
     cores = list(T.cores)
-    steps, info = _plan(cores, topo)
-    home, t_near, t_far, u_near, u_far, diag = info[r]
+    calls, place = _plan(cores, topo)
+    mine = place[r]
+    t_near, t_far, u_pair = mine[2], mine[3], mine[4]
 
     lands = {}
-    for step in steps:
-        for sender in step:
-            for tile, dst, m in step[sender]:
+    for sender in calls:
+        for name in calls[sender]:
+            for tile, n, dst, m in calls[sender][name]:
                 if dst == r:
                     lands[tile] = len(_bits(m))
 
-    def codes(j, n=1):
-        return T.q[:, j * W:(j + n) * W]
+    def cols(k, n=1):
+        return slice(k * W, (k + n) * W)
 
-    def plane(j, n=1):
-        return T.s[:, j * W:(j + n) * W]
+    me = mine.index(r)
 
     g.sync.dma_start(T.xb[:], T.x[:]).then_inc(T.sem.ld, 16)
     g.vector.wait_ge(T.sem.ld, 16)
-    g.vector.quantize_mx(codes(r), plane(r), T.xb[:]).then_inc(T.sem.qd, 1)
+    g.vector.quantize_mx(T.q[:, cols(me)], T.s[:, cols(me)], T.xb[:]).then_inc(T.sem.qd, 1)
 
-    left = [0]
+    left = {"sent": 0, "gone": 0}
 
-    def send(step, what):
+    def send(name, what, sem="sent"):
         trs = []
-        for tile, dst, m in steps[step][r]:
+        for tile, n, dst, m in calls[r][name]:
             rid, pid = topo.addr(cores[dst], core)
+            a, b = cols(mine.index(tile), n), cols(place[dst].index(tile), n)
             if what == "c":
-                ap = codes(tile).bitcast(dt.uint8)
+                src, out = T.q[:, a].bitcast(dt.uint8), T.q[:, b].bitcast(dt.uint8)
             else:
-                ap = plane(tile)
+                src, out = T.s[:, a], T.s[:, b]
             trs.append(RemoteDMATransfer(dst_ids=[DstId(rid=rid, pnc=pid)], dma_engine_mask=m,
-                                         remote_sem=T.sem["%s%d" % (what, tile)], src=ap, dst=ap))
-            left[0] += len(_bits(m))
-        g.remote_dma_fused(trs, local_sem=T.sem.sent)
+                                         remote_sem=T.sem["%s%d" % (what, tile)], src=src, dst=out))
+            left[sem] += len(_bits(m))
+        g.remote_dma_fused(trs, local_sem=T.sem[sem])
 
     g.wait_ge(T.sem.qd, 1)
-    send(0, "c")
-    send(0, "p")
+    send("own_out", "c")
+    send("own_out", "p")
+    send("own_chip", "c")
+    send("own_chip", "p")
     for what in ("c", "p"):
-        for t in (t_near, t_far):
-            g.wait_ge(T.sem["%s%d" % (what, t)], lands[t])
-        send(1, what)
-    g.wait_ge(T.sem.sent, left[0])
+        leaves = "gone" if what == "c" else "sent"
+        g.wait_ge(T.sem["%s%d" % (what, t_near)], lands[t_near])
+        send("relay_cable", what, leaves)
+        g.wait_ge(T.sem["%s%d" % (what, t_far)], lands[t_far])
+        send("relay_switch", what, leaves)
+        send("pair_chip", what)
+    g.wait_ge(T.sem.sent, left["sent"])
 
-    def merged(pair):
-        return [pair] if pair[1] == pair[0] + 1 else [[pair[0]], [pair[1]]]
-
-    groups = merged(home) + [[t_near], [t_far], [u_near], [u_far]] + merged(diag)
-    stores = {"st_a": 0, "st_b": 0}
+    peer = [j for j in mine[0:2] if j != r][0]
+    groups = [(0, 2, [peer]), (2, 2, [t_near, t_far]), (4, 2, [u_pair]), (6, 1, [mine[6]]), (7, 1, [mine[7]])]
     g.tensor.wait_ge(T.sem.qd, 1)
-    for k, tiles in enumerate(groups):
-        a, n = tiles[0], len(tiles)
-        for j in tiles:
-            if j != r:
-                g.tensor.wait_ge(T.sem["c%d" % j], lands[j])
-                g.tensor.wait_ge(T.sem["p%d" % j], lands[j])
-        bank = T.ps[:, 512 * k:512 * k + n * W]
-        g.tensor.matmul_mx(bank, codes(r), plane(r), codes(a, n), plane(a, n), True, True).then_inc(T.sem["mm%d" % k], 1)
+    for k, (a, n, awaited) in enumerate(groups):
+        for j in awaited:
+            g.tensor.wait_ge(T.sem["c%d" % j], lands[j])
+            g.tensor.wait_ge(T.sem["p%d" % j], lands[j])
+        g.tensor.matmul_mx(T.ps[:, 512 * k:512 * k + n * W], T.q[:, cols(me)], T.s[:, cols(me)],
+                           T.q[:, cols(a, n)], T.s[:, cols(a, n)], True, True).then_inc(T.sem["mm%d" % k], 1)
+
+    for k, (a, n, awaited) in enumerate(groups[:4]):
         g.vector.wait_ge(T.sem["mm%d" % k], 1)
-        g.vector.tensor_copy(T.yb[:, a * W:(a + n) * W], bank).then_inc(T.sem["cp%d" % k], 1)
-        queue, name = ((g.sync, "st_a"), (g.scalar, "st_b"))[k % 2]
-        queue.wait_ge(T.sem["cp%d" % k], 1)
-        queue.dma_start(T.y[:, a * W:(a + n) * W], T.yb[:, a * W:(a + n) * W]).then_inc(T.sem[name], 16)
-        stores[name] += 16
-    g.sync.wait_ge(T.sem.st_a, stores["st_a"])
-    g.scalar.wait_ge(T.sem.st_b, stores["st_b"])
+        g.vector.tensor_copy(T.yb[:, cols(a, n)], T.ps[:, 512 * k:512 * k + n * W]).then_inc(T.sem["cp%d" % k], 1)
+
+    def store(queue, sem, a, n):
+        queue.dma_start(T.y[:, cols(mine[a], n)], T.yb[:, cols(a, n)]).then_inc(sem, 16)
+
+    g.sync.wait_ge(T.sem.gone, left["gone"])
+    g.scalar.wait_ge(T.sem.gone, left["gone"])
+    g.sync.wait_ge(T.sem.cp0, 1)
+    store(g.sync, T.sem.st_a, 0, 2)
+    g.sync.wait_ge(T.sem.cp1, 1)
+    store(g.sync, T.sem.st_a, 2, 1)
+    g.scalar.wait_ge(T.sem.cp1, 1)
+    store(g.scalar, T.sem.st_b, 3, 1)
+    g.sync.wait_ge(T.sem.cp2, 1)
+    store(g.sync, T.sem.st_a, 4, 1)
+    store(g.sync, T.sem.st_a, 5, 1)
+    g.scalar.wait_ge(T.sem.mm4, 1)
+    g.scalar.activation(T.yb[:, cols(7)], T.ps[:, 512 * 4:512 * 4 + W], ActivationFunctionType.Copy).then_inc(T.sem.cp4, 1)
+    g.scalar.wait_ge(T.sem.cp3, 1)
+    g.scalar.wait_ge(T.sem.cp4, 1)
+    store(g.scalar, T.sem.st_b, 6, 2)
+    g.sync.wait_ge(T.sem.st_a, 16 * 4)
+    g.scalar.wait_ge(T.sem.st_b, 16 * 2)

@@ -16,6 +16,9 @@ SEMAPHORES = (["ld", "qd", "sent", "gone", "st_a", "st_b"]
               + ["c%d" % j for j in range(N)] + ["p%d" % j for j in range(N)]
               + ["mm%d" % k for k in range(NG)] + ["cp%d" % k for k in range(NG)])
 
+CARRIES = {"far": "cp", "near": "cp", "own_chip": "cp", "relay_cable": "c", "relay_switch": "cp",
+           "pair_chip": "cp", "diag_chip": "p"}
+
 
 def _bits(m):
     return [e for e in range(m.bit_length()) if (m >> e) & 1]
@@ -46,11 +49,13 @@ def _plan(cores, topo):
         m_near, m_far, m_stay = _mask(leave[0::2]), _mask(leave[1::2]), _mask(stay)
         t_near, t_far = by_host[near][slot], by_host[far][slot]
         calls[r] = {
-            "own_out": [(r, 1, t_near, m_near), (r, 1, t_far, m_far)],
-            "own_chip": [(r, 1, peer, m_stay)],
-            "relay_cable": [(t_near, 1, t_far, m_far)],
-            "relay_switch": [(t_far, 1, by_host[near][1 - slot], m_near)],
-            "pair_chip": [(t_near, 2, peer, m_stay)],
+            "far": (r, 1, t_far, m_far),
+            "near": (r, 1, t_near, m_near),
+            "own_chip": (r, 1, peer, m_stay),
+            "relay_cable": (t_near, 1, t_far, m_far),
+            "relay_switch": (t_far, 1, by_host[near][1 - slot], m_near),
+            "pair_chip": (t_near, 2, peer, m_stay),
+            "diag_chip": (by_host[diag][1 - slot], 1, peer, m_stay),
         }
         place[r] = (sorted(by_host[h]) + [t_near, t_far, by_host[near][1 - slot], by_host[far][1 - slot]]
                     + sorted(by_host[diag]))
@@ -65,13 +70,16 @@ def rank_program(g, core, T, topo):
     calls, place = _plan(cores, topo)
     mine = place[r]
     t_near, t_far, u_pair = mine[2], mine[3], mine[4]
+    d_switch = calls[r]["diag_chip"][0]
+    d_cable = [j for j in mine[6:8] if j != d_switch][0]
 
     lands = {}
     for sender in calls:
         for name in calls[sender]:
-            for tile, n, dst, m in calls[sender][name]:
-                if dst == r:
-                    lands[tile] = len(_bits(m))
+            tile, n, dst, m = calls[sender][name]
+            if dst == r:
+                for what in CARRIES[name]:
+                    lands[what, tile] = len(_bits(m))
 
     def cols(k, n=1):
         return slice(k * W, (k + n) * W)
@@ -85,40 +93,49 @@ def rank_program(g, core, T, topo):
     left = {"sent": 0, "gone": 0}
 
     def send(name, what, sem="sent"):
-        trs = []
-        for tile, n, dst, m in calls[r][name]:
-            rid, pid = topo.addr(cores[dst], core)
-            a, b = cols(mine.index(tile), n), cols(place[dst].index(tile), n)
-            if what == "c":
-                src, out = T.q[:, a].bitcast(dt.uint8), T.q[:, b].bitcast(dt.uint8)
-            else:
-                src, out = T.s[:, a], T.s[:, b]
-            trs.append(RemoteDMATransfer(dst_ids=[DstId(rid=rid, pnc=pid)], dma_engine_mask=m,
-                                         remote_sem=T.sem["%s%d" % (what, tile)], src=src, dst=out))
-            left[sem] += len(_bits(m))
-        g.remote_dma_fused(trs, local_sem=T.sem[sem])
+        tile, n, dst, m = calls[r][name]
+        rid, pid = topo.addr(cores[dst], core)
+        a, b = cols(mine.index(tile), n), cols(place[dst].index(tile), n)
+        if what == "c":
+            src, out = T.q[:, a].bitcast(dt.uint8), T.q[:, b].bitcast(dt.uint8)
+        else:
+            src, out = T.s[:, a], T.s[:, b]
+        left[sem] += len(_bits(m))
+        g.remote_dma_fused([RemoteDMATransfer(dst_ids=[DstId(rid=rid, pnc=pid)], dma_engine_mask=m,
+                                              remote_sem=T.sem["%s%d" % (what, tile)], src=src, dst=out)],
+                           local_sem=T.sem[sem])
+
+    def arrived(queue, what, tile):
+        queue.wait_ge(T.sem["%s%d" % (what, tile)], lands[what, tile])
 
     g.wait_ge(T.sem.qd, 1)
-    send("own_out", "c")
-    send("own_out", "p")
+    send("far", "p")
+    send("far", "c")
+    send("near", "c")
     send("own_chip", "c")
     send("own_chip", "p")
-    for what in ("c", "p"):
-        leaves = "gone" if what == "c" else "sent"
-        g.wait_ge(T.sem["%s%d" % (what, t_near)], lands[t_near])
-        send("relay_cable", what, leaves)
-        g.wait_ge(T.sem["%s%d" % (what, t_far)], lands[t_far])
-        send("relay_switch", what, leaves)
-        send("pair_chip", what)
+    arrived(g, "p", t_far)
+    send("relay_switch", "p")
+    send("near", "p")
+    arrived(g, "c", t_near)
+    send("relay_cable", "c", "gone")
+    arrived(g, "c", t_far)
+    send("relay_switch", "c", "gone")
+    arrived(g, "p", d_switch)
+    send("diag_chip", "p")
+    send("pair_chip", "c")
+    arrived(g, "p", t_near)
+    send("pair_chip", "p")
     g.wait_ge(T.sem.sent, left["sent"])
 
     peer = [j for j in mine[0:2] if j != r][0]
-    groups = [(0, 2, [peer]), (2, 2, [t_near, t_far]), (4, 2, [u_pair]), (6, 1, [mine[6]]), (7, 1, [mine[7]])]
+    groups = [(0, 2, [peer]), (2, 2, [t_near, t_far]), (4, 2, [u_pair]),
+              (mine.index(d_switch), 1, [d_switch]), (mine.index(d_cable), 1, [d_cable])]
     g.tensor.wait_ge(T.sem.qd, 1)
     for k, (a, n, awaited) in enumerate(groups):
         for j in awaited:
-            g.tensor.wait_ge(T.sem["c%d" % j], lands[j])
-            g.tensor.wait_ge(T.sem["p%d" % j], lands[j])
+            arrived(g.tensor, "c", j)
+            arrived(g.tensor, "p", j)
         g.tensor.matmul_mx(T.ps[:, 512 * k:512 * k + n * W], T.q[:, cols(me)], T.s[:, cols(me)],
                            T.q[:, cols(a, n)], T.s[:, cols(a, n)], True, True).then_inc(T.sem["mm%d" % k], 1)
 
@@ -140,8 +157,10 @@ def rank_program(g, core, T, topo):
     g.sync.wait_ge(T.sem.cp2, 1)
     store(g.sync, T.sem.st_a, 4, 1)
     store(g.sync, T.sem.st_a, 5, 1)
+    a_last = groups[4][0]
     g.scalar.wait_ge(T.sem.mm4, 1)
-    g.scalar.activation(T.yb[:, cols(7)], T.ps[:, 512 * 4:512 * 4 + W], ActivationFunctionType.Copy).then_inc(T.sem.cp4, 1)
+    g.scalar.activation(T.yb[:, cols(a_last)], T.ps[:, 512 * 4:512 * 4 + W],
+                        ActivationFunctionType.Copy).then_inc(T.sem.cp4, 1)
     g.scalar.wait_ge(T.sem.cp3, 1)
     g.scalar.wait_ge(T.sem.cp4, 1)
     store(g.scalar, T.sem.st_b, 6, 2)

from concourse.bass import DstId, RemoteDMATransfer
from concourse.mybir import dt, ActivationFunctionType

N = 8
W = 128
NG = 5

SCRATCH = {
    "xb": ("sbuf", [128, 4 * W], "bfloat16"),
    "q": ("sbuf", [128, N * W], "float8_e4m3fn_x4"),
    "s": ("sbuf", [128, N * W], "uint8"),
    "ps": ("psum", [128, 512 * NG], "float32"),
    "yb": ("sbuf", [128, N * W], "float32"),
}
SEMAPHORES = (["ld", "qd", "sent", "gone", "st_a", "st_b"]
              + ["c%d" % j for j in range(N)] + ["p%d" % j for j in range(N)]
              + ["mm%d" % k for k in range(NG)] + ["cp%d" % k for k in range(NG)])

CARRIES = {"far": "cp", "near": "cp", "own_chip": "cp", "relay_cable": "c", "relay_switch": "cp",
           "pair_chip": "cp", "diag_chip": "p"}


def _bits(m):
    return [e for e in range(m.bit_length()) if (m >> e) & 1]


def _mask(engines):
    m = 0
    for e in engines:
        m |= 1 << e
    return m


def _plan(cores, topo):
    by_host = {}
    for r, c in enumerate(cores):
        by_host.setdefault(topo.host(c), []).append(r)
    calls, place = {}, {}
    for r, c in enumerate(cores):
        h = topo.host(c)
        slot = by_host[h].index(r)
        peer = by_host[h][1 - slot]
        open_to = [k for k in by_host if k != h and topo.may_write(c, cores[by_host[k][slot]])]
        near = [k for k in open_to if topo.rack(k) == topo.rack(h)][0]
        far = [k for k in open_to if topo.rack(k) != topo.rack(h)][0]
        diag = [k for k in by_host if k not in (h, near, far)][0]
        leave = _bits(topo.mask(c, cores[by_host[near][slot]]) & topo.mask(c, cores[by_host[far][slot]]))
        stay = [e for e in _bits(topo.mask(c, cores[peer])) if e not in leave]
        m_near, m_far, m_stay = _mask(leave[0::2]), _mask(leave[1::2]), _mask(stay)
        t_near, t_far = by_host[near][slot], by_host[far][slot]
        calls[r] = {
            "far": (r, 1, t_far, m_far),
            "near": (r, 1, t_near, m_near),
            "own_chip": (r, 1, peer, m_stay),
            "relay_cable": (t_near, 1, t_far, m_far),
            "relay_switch": (t_far, 1, by_host[near][1 - slot], m_near),
            "pair_chip": (t_near, 2, peer, m_stay),
            "diag_chip": (by_host[diag][1 - slot], 1, peer, m_stay),
        }
        place[r] = (sorted(by_host[h]) + [t_near, t_far, by_host[near][1 - slot], by_host[far][1 - slot]]
                    + sorted(by_host[diag]))
    return calls, place


def rank_program(g, core, T, topo):
    r = T.rank_of(core)
    if r is None:
        return
    cores = list(T.cores)
    calls, place = _plan(cores, topo)
    mine = place[r]
    t_near, t_far, u_pair = mine[2], mine[3], mine[4]
    d_switch = calls[r]["diag_chip"][0]
    d_cable = [j for j in mine[6:8] if j != d_switch][0]

    lands = {}
    for sender in calls:
        for name in calls[sender]:
            tile, n, dst, m = calls[sender][name]
            if dst == r:
                for what in CARRIES[name]:
                    lands[what, tile] = len(_bits(m))

    def cols(k, n=1):
        return slice(k * W, (k + n) * W)

    me = mine.index(r)

    g.sync.dma_start(T.xb[:], T.x[:]).then_inc(T.sem.ld, 16)
    g.vector.wait_ge(T.sem.ld, 16)
    g.vector.quantize_mx(T.q[:, cols(me)], T.s[:, cols(me)], T.xb[:]).then_inc(T.sem.qd, 1)

    left = {"sent": 0, "gone": 0}

    def send(name, what, sem="sent"):
        tile, n, dst, m = calls[r][name]
        rid, pid = topo.addr(cores[dst], core)
        a, b = cols(mine.index(tile), n), cols(place[dst].index(tile), n)
        if what == "c":
            src, out = T.q[:, a].bitcast(dt.uint8), T.q[:, b].bitcast(dt.uint8)
        else:
            src, out = T.s[:, a], T.s[:, b]
        left[sem] += len(_bits(m))
        g.remote_dma_fused([RemoteDMATransfer(dst_ids=[DstId(rid=rid, pnc=pid)], dma_engine_mask=m,
                                              remote_sem=T.sem["%s%d" % (what, tile)], src=src, dst=out)],
                           local_sem=T.sem[sem])

    def arrived(queue, what, tile):
        queue.wait_ge(T.sem["%s%d" % (what, tile)], lands[what, tile])

    g.wait_ge(T.sem.qd, 1)
    send("far", "p")
    send("far", "c")
    send("near", "c")
    send("own_chip", "c")
    send("own_chip", "p")
    arrived(g, "p", t_far)
    send("relay_switch", "p")
    send("near", "p")
    arrived(g, "c", t_near)
    send("relay_cable", "c", "gone")
    arrived(g, "c", t_far)
    send("relay_switch", "c", "gone")
    arrived(g, "p", d_switch)
    send("diag_chip", "p")
    send("pair_chip", "c")
    arrived(g, "p", t_near)
    send("pair_chip", "p")
    g.wait_ge(T.sem.sent, left["sent"])

    peer = [j for j in mine[0:2] if j != r][0]
    groups = [(0, 2, [peer]), (2, 2, [t_near, t_far]), (4, 2, [u_pair]),
              (mine.index(d_switch), 1, [d_switch]), (mine.index(d_cable), 1, [d_cable])]
    g.tensor.wait_ge(T.sem.qd, 1)
    for k, (a, n, awaited) in enumerate(groups):
        for j in awaited:
            arrived(g.tensor, "c", j)
            arrived(g.tensor, "p", j)
        g.tensor.matmul_mx(T.ps[:, 512 * k:512 * k + n * W], T.q[:, cols(me)], T.s[:, cols(me)],
                           T.q[:, cols(a, n)], T.s[:, cols(a, n)], True, True).then_inc(T.sem["mm%d" % k], 1)

    for k, (a, n, awaited) in enumerate(groups[:4]):
        g.vector.wait_ge(T.sem["mm%d" % k], 1)
        g.vector.tensor_copy(T.yb[:, cols(a, n)], T.ps[:, 512 * k:512 * k + n * W]).then_inc(T.sem["cp%d" % k], 1)

    def store(queue, sem, a, n):
        queue.dma_start(T.y[:, cols(mine[a], n)], T.yb[:, cols(a, n)]).then_inc(sem, 16)

    g.sync.wait_ge(T.sem.gone, left["gone"])
    g.scalar.wait_ge(T.sem.gone, left["gone"])
    g.sync.wait_ge(T.sem.cp0, 1)
    store(g.sync, T.sem.st_a, 0, 2)
    g.sync.wait_ge(T.sem.cp1, 1)
    store(g.sync, T.sem.st_a, 2, 1)
    g.scalar.wait_ge(T.sem.cp1, 1)
    store(g.scalar, T.sem.st_b, 3, 1)
    g.sync.wait_ge(T.sem.cp2, 1)
    store(g.sync, T.sem.st_a, 4, 1)
    store(g.sync, T.sem.st_a, 5, 1)
    a_last = groups[4][0]
    g.scalar.wait_ge(T.sem.mm4, 1)
    g.scalar.activation(T.yb[:, cols(a_last)], T.ps[:, 512 * 4:512 * 4 + W],
                        ActivationFunctionType.Copy).then_inc(T.sem.cp4, 1)
    g.scalar.wait_ge(T.sem.cp3, 1)
    g.scalar.wait_ge(T.sem.cp4, 1)
    store(g.scalar, T.sem.st_b, 6, 2)
    g.sync.wait_ge(T.sem.st_a, 16 * 4)
    g.scalar.wait_ge(T.sem.st_b, 16 * 2)
